import numpy as np
import ml_dtypes

BF16 = ml_dtypes.bfloat16


def bf(x):
    return np.asarray(x, np.float32).astype(BF16)


def f32(x):
    return np.asarray(x, np.float32)


def f64(x):
    return np.asarray(x).astype(np.float64)


def striped(idx):
    return np.tile(idx.reshape(-1, 16).T, (8, 1))


S, K, N, V, D, H, O = 1024, 256, 1024, 512, 2, 256, 512


def gelu_tanh(v):
    return 0.5 * v * (1.0 + np.tanh(np.sqrt(2.0 / np.pi) * (v + 0.044715 * v**3)))


def setup_inputs():
    return {"table": bf(np.random.standard_normal((K, S))), "w": bf(np.random.standard_normal((D, K, H)) / np.sqrt(D * K)), "b": f32(0.5 * np.random.standard_normal((H, 1))), "w2": bf(np.random.standard_normal((H, O)) / np.sqrt(H)), "offs": striped(np.random.permutation(np.tile(np.arange(S), 2))[:N])}


def reference(table, w, b, w2, offs):
    idx = offs[:16].T.reshape(-1)
    x = f64(table)[:, idx]
    t = sum(f64(w)[d].T @ x[:, d * V : (d + 1) * V] for d in range(D)) + f64(b)
    t = gelu_tanh(t)
    return f64(w2).T @ t

@@ -1,0 +1,86 @@
+import concourse.mybir as mybir
+
+BF16 = mybir.dt.bfloat16
+F32 = mybir.dt.float32
+U16 = mybir.dt.uint16
+GELU = mybir.ActivationFunctionType.Gelu_apprx_tanh
+
+P = 128
+LIST_ROWS = 16
+EDGE_PARTS = 2
+
+FLOPS = 2 * 2 * 256 * 256 * 512 + 2 * 256 * 512 * 512
+
+
+def tile_rows_edge2_gelu_rep_kernel(tc, table, w, b, w2, offs, out):
+    nc = tc.nc
+    features, nodes = table.shape
+    ends, hidden = w.shape[0], w.shape[2]
+    outputs, edges = out.shape
+    k_blocks, h_blocks, o_blocks = features // P, hidden // P, outputs // P
+    part_edges = edges // EDGE_PARTS
+
+    table_blocks = table.rearrange("(p a) s -> a p s", a=k_blocks)
+    w_ends = w.rearrange("d (p a) i -> d p (a i)", a=k_blocks)
+
+    with (
+        tc.tile_pool(name="held", bufs=1) as held,
+        tc.psum_pool(name="psum", bufs=8) as psum,
+    ):
+        node_tiles = [held.tile([P, nodes], BF16, name=f"nodes{a}") for a in range(k_blocks)]
+        w_tiles = [held.tile([P, k_blocks * hidden], BF16, name=f"w_end{d}") for d in range(ends)]
+        offsets = held.tile(list(offs.shape), U16, name="offsets")
+        bias = held.tile([P, h_blocks], F32, name="bias")
+        w2_tile = held.tile([P, h_blocks, outputs], BF16, name="w2_tile")
+
+        nc.sync.dma_start(node_tiles[0][:], table_blocks[0])
+        nc.scalar.dma_start(w_tiles[0][:], w_ends[0])
+        nc.sync.dma_start(offsets[:], offs)
+        nc.sync.dma_start(w_tiles[1][:], w_ends[1])
+        nc.sync.dma_start(node_tiles[1][:], table_blocks[1])
+        nc.sync.dma_start(bias[:], b.rearrange("(m p) o -> p (m o)", p=P))
+        nc.sync.dma_start(w2_tile[:], w2.rearrange("(m p) o -> p m o", p=P))
+
+        pre_banks = {
+            (part, m): psum.tile([P, part_edges], F32, name=f"pre{part}{m}", tag="bank")
+            for part in range(EDGE_PARTS)
+            for m in range(h_blocks)
+        }
+
+        def gathered_matmul(part, m, d, a):
+            first = (d * edges + part * part_edges) // LIST_ROWS
+            picked = node_tiles[a][:].indirect(offsets[:, first : first + part_edges // LIST_ROWS])
+            weights = w_tiles[d][:, a * hidden + m * P : a * hidden + (m + 1) * P]
+            nc.tensor.matmul(
+                pre_banks[part, m][:], weights, picked,
+                start=(a == 0 and d == 0), stop=(a == k_blocks - 1 and d == ends - 1),
+            )
+
+        for d in range(ends):
+            for part in range(EDGE_PARTS):
+                for m in range(h_blocks):
+                    gathered_matmul(part, m, d, 0)
+        h_tiles = {}
+        for part in range(EDGE_PARTS):
+            for m in range(h_blocks):
+                for d in range(ends):
+                    gathered_matmul(part, m, d, 1)
+                h_tiles[part, m] = held.tile([P, part_edges], BF16, name=f"h{part}{m}")
+                nc.scalar.activation(h_tiles[part, m][:], pre_banks[part, m][:], GELU, bias=bias[:, m : m + 1])
+
+        for part in range(EDGE_PARTS):
+            for o in range(o_blocks):
+                out_bank = psum.tile([P, part_edges], F32, name=f"post{part}{o}", tag="bank")
+                for m in range(h_blocks):
+                    nc.tensor.matmul(
+                        out_bank[:], w2_tile[:, m, o * P : (o + 1) * P], h_tiles[part, m][:],
+                        start=(m == 0), stop=(m == h_blocks - 1),
+                    )
+                staged = held.tile([P, part_edges], F32, name=f"staged{part}{o}")
+                if o % 2 == 0:
+                    nc.vector.tensor_copy(staged[:], out_bank[:])
+                else:
+                    nc.scalar.copy(staged[:], out_bank[:])
+                nc.sync.dma_start(
+                    out[o * P : (o + 1) * P, part * part_edges : (part + 1) * part_edges], staged[:]
+                )

@@ -20,25 +20,26 @@ def tile_rows_edge2_gelu_rep_kernel(tc, table, w, b, w2, offs, out):
     k_blocks, h_blocks, o_blocks = features // P, hidden // P, outputs // P
     part_edges = edges // EDGE_PARTS
 
-    table_blocks = table.rearrange("(p a) s -> a p s", a=k_blocks)
-    w_ends = w.rearrange("d (p a) i -> d p (a i)", a=k_blocks)
+    table_blocks = table.rearrange("(a p) s -> a p s", p=P)
+    w_blocks = w.rearrange("d (a p) i -> a p d i", p=P)
 
     with (
         tc.tile_pool(name="held", bufs=1) as held,
         tc.psum_pool(name="psum", bufs=8) as psum,
     ):
         node_tiles = [held.tile([P, nodes], BF16, name=f"nodes{a}") for a in range(k_blocks)]
-        w_tiles = [held.tile([P, k_blocks * hidden], BF16, name=f"w_end{d}") for d in range(ends)]
+        w_tiles = [held.tile([P, ends, hidden], BF16, name=f"w_block{a}") for a in range(k_blocks)]
         offsets = held.tile(list(offs.shape), U16, name="offsets")
         bias = held.tile([P, h_blocks], F32, name="bias")
         w2_tile = held.tile([P, h_blocks, outputs], BF16, name="w2_tile")
 
         nc.sync.dma_start(node_tiles[0][:], table_blocks[0])
-        nc.scalar.dma_start(w_tiles[0][:], w_ends[0])
+        nc.scalar.dma_start(w_tiles[0][:, 0, :], w_blocks[0][:, 0, :])
         nc.sync.dma_start(offsets[:], offs)
-        nc.sync.dma_start(w_tiles[1][:], w_ends[1])
-        nc.sync.dma_start(node_tiles[1][:], table_blocks[1])
+        nc.sync.dma_start(w_tiles[0][:, 1, :], w_blocks[0][:, 1, :])
         nc.sync.dma_start(bias[:], b.rearrange("(m p) o -> p (m o)", p=P))
+        nc.sync.dma_start(node_tiles[1][:], table_blocks[1])
+        nc.sync.dma_start(w_tiles[1][:], w_blocks[1])
         nc.sync.dma_start(w2_tile[:], w2.rearrange("(m p) o -> p m o", p=P))
 
         pre_banks = {
@@ -50,7 +51,7 @@ def tile_rows_edge2_gelu_rep_kernel(tc, table, w, b, w2, offs, out):
         def gathered_matmul(part, m, d, a):
             first = (d * edges + part * part_edges) // LIST_ROWS
             picked = node_tiles[a][:].indirect(offsets[:, first : first + part_edges // LIST_ROWS])
-            weights = w_tiles[d][:, a * hidden + m * P : a * hidden + (m + 1) * P]
+            weights = w_tiles[a][:, d, m * P : (m + 1) * P]
             nc.tensor.matmul(
                 pre_banks[part, m][:], weights, picked,
                 start=(a == 0 and d == 0), stop=(a == k_blocks - 1 and d == ends - 1),

@@ -69,19 +69,19 @@ def tile_rows_edge2_gelu_rep_kernel(tc, table, w, b, w2, offs, out):
                 h_tiles[part, m] = held.tile([P, part_edges], BF16, name=f"h{part}{m}")
                 nc.scalar.activation(h_tiles[part, m][:], pre_banks[part, m][:], GELU, bias=bias[:, m : m + 1])
 
+        half_edges = part_edges // 2
         for part in range(EDGE_PARTS):
             for o in range(o_blocks):
-                out_bank = psum.tile([P, part_edges], F32, name=f"post{part}{o}", tag="bank")
-                for m in range(h_blocks):
-                    nc.tensor.matmul(
-                        out_bank[:], w2_tile[:, m, o * P : (o + 1) * P], h_tiles[part, m][:],
-                        start=(m == 0), stop=(m == h_blocks - 1),
-                    )
                 staged = held.tile([P, part_edges], F32, name=f"staged{part}{o}")
-                if o % 2 == 0:
-                    nc.vector.tensor_copy(staged[:], out_bank[:])
-                else:
-                    nc.scalar.copy(staged[:], out_bank[:])
+                for half, copy in enumerate((nc.vector.tensor_copy, nc.scalar.copy)):
+                    columns = slice(half * half_edges, (half + 1) * half_edges)
+                    out_bank = psum.tile([P, half_edges], F32, name=f"post{part}{o}{half}", tag="bank")
+                    for m in range(h_blocks):
+                        nc.tensor.matmul(
+                            out_bank[:], w2_tile[:, m, o * P : (o + 1) * P], h_tiles[part, m][:, columns],
+                            start=(m == 0), stop=(m == h_blocks - 1),
+                        )
+                    copy(staged[:, columns], out_bank[:])
                 nc.sync.dma_start(
                     out[o * P : (o + 1) * P, part * part_edges : (part + 1) * part_edges], staged[:]
                 )

import concourse.mybir as mybir

BF16 = mybir.dt.bfloat16
F32 = mybir.dt.float32
U16 = mybir.dt.uint16
GELU = mybir.ActivationFunctionType.Gelu_apprx_tanh

P = 128
LIST_ROWS = 16
EDGE_PARTS = 2

FLOPS = 2 * 2 * 256 * 256 * 512 + 2 * 256 * 512 * 512


def tile_rows_edge2_gelu_rep_kernel(tc, table, w, b, w2, offs, out):
    nc = tc.nc
    features, nodes = table.shape
    ends, hidden = w.shape[0], w.shape[2]
    outputs, edges = out.shape
    k_blocks, h_blocks, o_blocks = features // P, hidden // P, outputs // P
    part_edges = edges // EDGE_PARTS

    table_blocks = table.rearrange("(a p) s -> a p s", p=P)
    w_blocks = w.rearrange("d (a p) i -> a p d i", p=P)

    with (
        tc.tile_pool(name="held", bufs=1) as held,
        tc.psum_pool(name="psum", bufs=8) as psum,
    ):
        node_tiles = [held.tile([P, nodes], BF16, name=f"nodes{a}") for a in range(k_blocks)]
        w_tiles = [held.tile([P, ends, hidden], BF16, name=f"w_block{a}") for a in range(k_blocks)]
        offsets = held.tile(list(offs.shape), U16, name="offsets")
        bias = held.tile([P, h_blocks], F32, name="bias")
        w2_tile = held.tile([P, h_blocks, outputs], BF16, name="w2_tile")

        nc.sync.dma_start(node_tiles[0][:], table_blocks[0])
        nc.scalar.dma_start(w_tiles[0][:, 0, :], w_blocks[0][:, 0, :])
        nc.sync.dma_start(offsets[:], offs)
        nc.sync.dma_start(w_tiles[0][:, 1, :], w_blocks[0][:, 1, :])
        nc.sync.dma_start(bias[:], b.rearrange("(m p) o -> p (m o)", p=P))
        nc.sync.dma_start(node_tiles[1][:], table_blocks[1])
        nc.sync.dma_start(w_tiles[1][:], w_blocks[1])
        nc.sync.dma_start(w2_tile[:], w2.rearrange("(m p) o -> p m o", p=P))

        pre_banks = {
            (part, m): psum.tile([P, part_edges], F32, name=f"pre{part}{m}", tag="bank")
            for part in range(EDGE_PARTS)
            for m in range(h_blocks)
        }

        def gathered_matmul(part, m, d, a):
            first = (d * edges + part * part_edges) // LIST_ROWS
            picked = node_tiles[a][:].indirect(offsets[:, first : first + part_edges // LIST_ROWS])
            weights = w_tiles[a][:, d, m * P : (m + 1) * P]
            nc.tensor.matmul(
                pre_banks[part, m][:], weights, picked,
                start=(a == 0 and d == 0), stop=(a == k_blocks - 1 and d == ends - 1),
            )

        for d in range(ends):
            for part in range(EDGE_PARTS):
                for m in range(h_blocks):
                    gathered_matmul(part, m, d, 0)
        h_tiles = {}
        for part in range(EDGE_PARTS):
            for m in range(h_blocks):
                for d in range(ends):
                    gathered_matmul(part, m, d, 1)
                h_tiles[part, m] = held.tile([P, part_edges], BF16, name=f"h{part}{m}")
                nc.scalar.activation(h_tiles[part, m][:], pre_banks[part, m][:], GELU, bias=bias[:, m : m + 1])

        half_edges = part_edges // 2
        for part in range(EDGE_PARTS):
            for o in range(o_blocks):
                staged = held.tile([P, part_edges], F32, name=f"staged{part}{o}")
                for half, copy in enumerate((nc.vector.tensor_copy, nc.scalar.copy)):
                    columns = slice(half * half_edges, (half + 1) * half_edges)
                    out_bank = psum.tile([P, half_edges], F32, name=f"post{part}{o}{half}", tag="bank")
                    for m in range(h_blocks):
                        nc.tensor.matmul(
                            out_bank[:], w2_tile[:, m, o * P : (o + 1) * P], h_tiles[part, m][:, columns],
                            start=(m == 0), stop=(m == h_blocks - 1),
                        )
                    copy(staged[:, columns], out_bank[:])
                nc.sync.dma_start(
                    out[o * P : (o + 1) * P, part * part_edges : (part + 1) * part_edges], staged[:]
                )
